import numpy as np
CORES = [4,12,20,28,36,44,52,60,132,140,148,156,164,172,180,188]
N = 16
T = 32
ROUTE = [[[11],[0],[7],[0],[12],[11],[2],[13],[9],[10],[3],[4],[3],[8],[11],[0],[4],[2],[1],[11],[8],[1],[12],[5],[9],[9],[12],[10],[6],[6],[14],[5]],[[4],[12],[13],[7],[7],[3],[2],[14],[8],[13],[3],[9],[6],[5],[12],[10],[14],[2],[15],[13],[14],[11],[4],[14],[8],[4],[7],[5],[9],[9],[2],[9]],[[3],[9],[13],[7],[13],[9],[11],[14],[2],[2],[1],[10],[13],[10],[5],[5],[13],[10],[15],[11],[8],[0],[8],[1],[5],[8],[3],[8],[2],[14],[4],[8]],[[4],[14],[5],[11],[12],[4],[3],[14],[10],[5],[4],[8],[14],[14],[0],[13],[14],[15],[12],[5],[4],[2],[12],[12],[9],[5],[14],[14],[6],[13],[9],[14]],[[8],[3],[7],[4],[9],[3],[8],[0],[3],[14],[15],[15],[9],[7],[11],[3],[10],[10],[9],[11],[1],[10],[9],[5],[12],[14],[1],[0],[2],[3],[12],[3]],[[8],[13],[1],[5],[14],[12],[3],[14],[9],[5],[1],[7],[13],[11],[6],[10],[3],[14],[12],[5],[7],[6],[2],[7],[1],[0],[8],[11],[7],[10],[9],[11]],[[14],[5],[9],[14],[8],[10],[11],[14],[7],[2],[1],[4],[7],[11],[11],[15],[13],[3],[6],[15],[5],[8],[4],[2],[15],[5],[8],[10],[4],[8],[12],[3]],[[11],[15],[14],[8],[2],[3],[12],[6],[3],[5],[2],[11],[9],[0],[0],[0],[9],[8],[8],[1],[6],[15],[5],[4],[6],[4],[4],[12],[8],[10],[9],[6]],[[10],[2],[12],[9],[3],[3],[2],[9],[4],[15],[15],[0],[1],[11],[8],[12],[2],[0],[6],[3],[0],[13],[14],[13],[3],[3],[2],[15],[11],[7],[0],[2]],[[14],[8],[13],[5],[13],[7],[13],[6],[4],[7],[1],[3],[13],[4],[6],[7],[15],[10],[3],[15],[0],[3],[11],[2],[12],[10],[13],[12],[10],[7],[1],[1]],[[11],[13],[11],[8],[3],[12],[15],[13],[9],[6],[1],[11],[11],[9],[7],[13],[12],[11],[10],[15],[6],[12],[8],[5],[7],[5],[3],[11],[7],[5],[4],[9]],[[5],[4],[12],[0],[14],[15],[8],[10],[10],[11],[9],[9],[12],[5],[3],[7],[15],[14],[12],[8],[12],[8],[11],[5],[2],[5],[0],[4],[0],[13],[7],[15]],[[7],[1],[9],[10],[2],[7],[8],[0],[7],[11],[13],[13],[13],[9],[10],[15],[2],[12],[11],[10],[6],[5],[3],[15],[10],[2],[1],[9],[15],[9],[14],[10]],[[8],[12],[5],[13],[2],[10],[14],[5],[14],[1],[11],[6],[8],[5],[13],[4],[0],[15],[1],[15],[13],[0],[13],[10],[8],[0],[0],[10],[11],[2],[4],[13]],[[7],[6],[12],[0],[5],[6],[13],[12],[9],[9],[15],[12],[2],[9],[14],[5],[10],[13],[11],[3],[5],[4],[1],[4],[1],[0],[4],[10],[11],[5],[10],[10]],[[5],[15],[7],[7],[9],[13],[12],[0],[15],[6],[4],[8],[7],[12],[2],[6],[14],[4],[0],[15],[7],[10],[3],[5],[9],[2],[11],[13],[13],[15],[6],[13]]]
ZW = 38
def setup_inputs(rng):
    return {"z": rng.standard_normal((N, 128, ZW), dtype=np.float32)}
def reference(z):
    y = np.zeros((N, 128, T), np.float64)
    fill = [0] * N
    for r in range(N):
        for t in range(T):
            for e in ROUTE[r][t]:
                y[r][:, t] += z[e][:, fill[e]].astype(np.float64)
                fill[e] += 1
    return {"y": y.astype(z.dtype)}

@@ -1,0 +1,227 @@
+import concourse.bass as bass
+
+ZCOLS = 38
+TOK = 32
+
+SCRATCH = {
+    "zs": ("sbuf", [128, ZCOLS], "float32"),
+    "stage": ("sbuf", [128, TOK], "float32"),
+}
+SEMAPHORES = ["loaded", "got", "sent", "arrived", "stored"]
+
+CAP = 4
+MAX_HELPERS = 8
+USE_IDLE = True
+SPLIT_CALLS = True
+
+PLAN = {}
+
+
+def next_pow2(n):
+    p = 1
+    while p < n:
+        p *= 2
+    return p
+
+
+def chunks(seq, sizes):
+    out, i = [], 0
+    for s in sizes:
+        out.append(list(seq[i:i + s]))
+        i += s
+    return out
+
+
+def even_sizes(n, parts, cap):
+    use = min(n, parts * cap)
+    sizes = [use // parts + (1 if i < use % parts else 0) for i in range(parts)] if parts else []
+    return sizes, n - use
+
+
+def masks_for(n, engines):
+    base = len(engines) // next_pow2(n)
+    cnt = [base] * n
+    spare = len(engines) - base * n
+    for i in range(n):
+        if spare >= cnt[i]:
+            spare -= cnt[i]
+            cnt[i] *= 2
+    out, pos = [], 0
+    for c in cnt:
+        m = 0
+        for x in engines[pos:pos + c]:
+            m |= 1 << x
+        pos += c
+        out.append((m, c))
+    return out
+
+
+def span(toks):
+    ks = [x[0] for x in toks]
+    return (max(ks) - min(ks) + 1) if ks else 0
+
+
+def grow(toks, tok):
+    return span(toks + [tok]) - span(toks)
+
+
+def assign(e, toks, me):
+    base = me - 4
+    idle = base + 64
+    other = [x for x in toks if x[1] % 2 != e % 2]
+    same = [x for x in toks if x[1] % 2 == e % 2 and x[1] != e]
+    selfs = [x for x in toks if x[1] == e]
+    ports_on = [base + 6, base + 7, base + 2, base + 3]
+    rest_on = [base + 5, base + 0, base + 1]
+    ports_off = [idle + 6, idle + 7, idle + 2, idle + 3]
+    best = None
+    for a in range(len(rest_on), -1, -1):
+        for b in range(0, (MAX_HELPERS - 4 - a if USE_IDLE else 0) + 1):
+            load = {}
+            n_on = min(len(other), 4 * CAP) if b else len(other)
+            sz, dummy = even_sizes(n_on, 4, 99)
+            parts = chunks(other, sz)
+            for c, p in zip(ports_on, parts):
+                load[c] = p
+            over = other[n_on:]
+            keep = min(len(same), (1 + a) * CAP)
+            spill = len(same) - keep
+            pool = list(same)
+            moved = []
+            offs = ports_off[:b]
+            szo, left = even_sizes(len(over), b, CAP)
+            if left:
+                continue
+            for c, p in zip(offs, chunks(over, szo)):
+                load[c] = p
+            room = [c for c in ports_on + offs]
+            while spill > 0:
+                cand = [(len(load[c]) // 2 if c in offs else 0, grow(load[c], x), c, x)
+                        for c in room if len(load[c]) < CAP for x in pool]
+                if not cand:
+                    break
+                cand.sort()
+                c, x = cand[0][2], cand[0][3]
+                load[c] = load[c] + [x]
+                pool.remove(x)
+                moved.append(x)
+                spill -= 1
+            group = [me] + rest_on[:a]
+            szs, dummy = even_sizes(len(pool), len(group), 99)
+            if spill > 0:
+                szs = [CAP + spill] + [CAP] * a
+            for c, p in zip(group, chunks(pool, szs)):
+                load[c] = p
+            helpers = [c for c in ports_on + offs + rest_on[:a]]
+            back = {c: [] for c in helpers}
+            on_help = [c for c in helpers if c not in offs]
+            for x in selfs:
+                cand = [(len(back[c]) // 2, grow(load[c] + back[c], x), c) for c in on_help]
+                cand.sort()
+                back[cand[0][2]].append(x)
+            r1 = 128 // (16 // next_pow2(len(helpers)))
+            cost = 0
+            for c in helpers:
+                n = len(load[c])
+                t = r1 + 16 + (24 if c in offs else 0) + (16 * n if SPLIT_CALLS and n > CAP else (128 // (8 // next_pow2(n)) if n else 0))
+                cost = max(cost, t)
+            cost = max(cost, r1 + 16 * len(load[me]))
+            width = max(span(load[c] + back[c]) for c in helpers)
+            key = (cost, len(helpers), width)
+            if best is None or key < best[0]:
+                best = (key, load, back, helpers, offs)
+    return best
+
+
+def build(tables, cores):
+    route = tables["ROUTE"]
+    n = len(cores)
+    toks = [[] for i in range(n)]
+    for r in range(n):
+        for t in range(len(route[r])):
+            e = route[r][t][0]
+            toks[e].append((len(toks[e]), r, t))
+    hand = {}
+    got = {}
+    first = {}
+    calls = {}
+    arrive = {c: 0 for c in cores}
+    for e in range(n):
+        me = cores[e]
+        key, load, back, helpers, offs = assign(e, toks[e], me)
+        helpers = [c for c in helpers if load[c] or back[c]]
+        width = max(span(load[c] + back[c]) for c in helpers)
+        order = [c for c in helpers if c in offs] + [c for c in helpers if c not in offs]
+        ms = masks_for(len(order), list(range(16)))
+        hand[me] = []
+        for c, (m, cnt) in zip(order, ms):
+            k0 = min(min(x[0] for x in load[c] + back[c]), ZCOLS - width)
+            hand[me].append((c, k0, width, m))
+            got[c] = cnt
+            first[c] = k0
+        first[me] = 0
+        for c in [me] + helpers:
+            out = load[c]
+            bk = back.get(c, [])
+            cl = []
+            groups = [out]
+            if SPLIT_CALLS and len(out) > CAP:
+                groups = [out[i:i + CAP] for i in range(0, len(out), CAP)]
+            for gi, grp in enumerate(groups):
+                trs = []
+                if grp:
+                    for x, (m, cnt) in zip(grp, masks_for(len(grp), list(range(8)))):
+                        trs.append((cores[x[1]], x[0] - first[c], x[2], m, cnt))
+                if gi == 0 and bk:
+                    for x, (m, cnt) in zip(bk, masks_for(len(bk), list(range(8, 16)))):
+                        trs.append((cores[x[1]], x[0] - first[c], x[2], m, cnt))
+                if trs:
+                    cl.append(trs)
+            calls[c] = cl
+            for trs in cl:
+                for d, kk, t, m, cnt in trs:
+                    arrive[d] += cnt
+    return {"hand": hand, "got": got, "calls": calls, "arrive": arrive}
+
+
+def bits(m):
+    return bin(m).count("1")
+
+
+def rank_program(g, core, T, topo):
+    if "p" not in PLAN:
+        PLAN["p"] = build(T.tables, list(T.cores))
+    p = PLAN["p"]
+    rank = T.rank_of(core)
+    if rank is None and core not in p["calls"]:
+        return
+    sent = 0
+
+    if rank is not None:
+        g.dma_start(T.zs[:, :], T.z[:, :]).then_inc(T.sem.loaded, 16)
+        g.wait_ge(T.sem.loaded, 16)
+        trs = []
+        for c, k0, w, m in p["hand"][core]:
+            rid, pid = topo.addr(c, core)
+            trs.append(bass.RemoteDMATransfer(dst_ids=[bass.DstId(rid=rid, pnc=pid)], dma_engine_mask=m,
+                                              remote_sem=T.sem.got, src=T.zs[:, k0:k0 + w], dst=T.zs[:, 0:w]))
+            sent += bits(m)
+        g.remote_dma_fused(trs, local_sem=T.sem.sent)
+    else:
+        g.wait_ge(T.sem.got, p["got"][core])
+
+    for call in p["calls"][core]:
+        trs = []
+        for d, kk, t, m, cnt in call:
+            rid, pid = topo.addr(d, core)
+            trs.append(bass.RemoteDMATransfer(dst_ids=[bass.DstId(rid=rid, pnc=pid)], dma_engine_mask=m,
+                                              remote_sem=T.sem.arrived, src=T.zs[:, kk:kk + 1], dst=T.stage[:, t:t + 1]))
+            sent += cnt
+        g.remote_dma_fused(trs, local_sem=T.sem.sent)
+
+    if rank is not None:
+        g.wait_ge(T.sem.arrived, p["arrive"][core])
+        g.dma_start(T.y[:, :], T.stage[:, :]).then_inc(T.sem.stored, 16)
+    g.wait_ge(T.sem.sent, sent)
+    if rank is not None:
+        g.wait_ge(T.sem.stored, 16)

@@ -11,7 +11,7 @@ SEMAPHORES = ["loaded", "got", "sent", "arrived", "stored"]
 
 CAP = 4
 MAX_HELPERS = 8
-USE_IDLE = True
+USE_IDLE = False
 SPLIT_CALLS = True
 
 PLAN = {}

@@ -10,9 +10,6 @@ SCRATCH = {
 SEMAPHORES = ["loaded", "got", "sent", "arrived", "stored"]
 
 CAP = 4
-MAX_HELPERS = 8
-USE_IDLE = False
-SPLIT_CALLS = True
 
 PLAN = {}
 
@@ -32,10 +29,8 @@ def chunks(seq, sizes):
     return out
 
 
-def even_sizes(n, parts, cap):
-    use = min(n, parts * cap)
-    sizes = [use // parts + (1 if i < use % parts else 0) for i in range(parts)] if parts else []
-    return sizes, n - use
+def even_sizes(n, parts):
+    return [n // parts + (1 if i < n % parts else 0) for i in range(parts)]
 
 
 def masks_for(n, engines):
@@ -67,69 +62,48 @@ def grow(toks, tok):
 
 def assign(e, toks, me):
     base = me - 4
-    idle = base + 64
     other = [x for x in toks if x[1] % 2 != e % 2]
     same = [x for x in toks if x[1] % 2 == e % 2 and x[1] != e]
     selfs = [x for x in toks if x[1] == e]
-    ports_on = [base + 6, base + 7, base + 2, base + 3]
-    rest_on = [base + 5, base + 0, base + 1]
-    ports_off = [idle + 6, idle + 7, idle + 2, idle + 3]
+    ports = [base + c for c in [6, 7, 2, 3]]
     best = None
-    for a in range(len(rest_on), -1, -1):
-        for b in range(0, (MAX_HELPERS - 4 - a if USE_IDLE else 0) + 1):
-            load = {}
-            n_on = min(len(other), 4 * CAP) if b else len(other)
-            sz, dummy = even_sizes(n_on, 4, 99)
-            parts = chunks(other, sz)
-            for c, p in zip(ports_on, parts):
-                load[c] = p
-            over = other[n_on:]
-            keep = min(len(same), (1 + a) * CAP)
-            spill = len(same) - keep
-            pool = list(same)
-            moved = []
-            offs = ports_off[:b]
-            szo, left = even_sizes(len(over), b, CAP)
-            if left:
-                continue
-            for c, p in zip(offs, chunks(over, szo)):
-                load[c] = p
-            room = [c for c in ports_on + offs]
-            while spill > 0:
-                cand = [(len(load[c]) // 2 if c in offs else 0, grow(load[c], x), c, x)
-                        for c in room if len(load[c]) < CAP for x in pool]
-                if not cand:
-                    break
-                cand.sort()
-                c, x = cand[0][2], cand[0][3]
-                load[c] = load[c] + [x]
-                pool.remove(x)
-                moved.append(x)
-                spill -= 1
-            group = [me] + rest_on[:a]
-            szs, dummy = even_sizes(len(pool), len(group), 99)
-            if spill > 0:
-                szs = [CAP + spill] + [CAP] * a
-            for c, p in zip(group, chunks(pool, szs)):
-                load[c] = p
-            helpers = [c for c in ports_on + offs + rest_on[:a]]
-            back = {c: [] for c in helpers}
-            on_help = [c for c in helpers if c not in offs]
-            for x in selfs:
-                cand = [(len(back[c]) // 2, grow(load[c] + back[c], x), c) for c in on_help]
-                cand.sort()
-                back[cand[0][2]].append(x)
-            r1 = 128 // (16 // next_pow2(len(helpers)))
-            cost = 0
-            for c in helpers:
-                n = len(load[c])
-                t = r1 + 16 + (24 if c in offs else 0) + (16 * n if SPLIT_CALLS and n > CAP else (128 // (8 // next_pow2(n)) if n else 0))
-                cost = max(cost, t)
-            cost = max(cost, r1 + 16 * len(load[me]))
-            width = max(span(load[c] + back[c]) for c in helpers)
-            key = (cost, len(helpers), width)
-            if best is None or key < best[0]:
-                best = (key, load, back, helpers, offs)
+    for a in range(3, -1, -1):
+        plain = [base + c for c in [5, 0, 1][:a]]
+        load = {}
+        for c, p in zip(ports, chunks(other, even_sizes(len(other), 4))):
+            load[c] = p
+        spill = len(same) - min(len(same), (1 + a) * CAP)
+        pool = list(same)
+        while spill > 0:
+            cand = [(grow(load[c], x), c, x) for c in ports if len(load[c]) < CAP for x in pool]
+            if not cand:
+                break
+            cand.sort()
+            c, x = cand[0][1], cand[0][2]
+            load[c] = load[c] + [x]
+            pool.remove(x)
+            spill -= 1
+        group = [me] + plain
+        szs = even_sizes(len(pool), len(group))
+        if spill > 0:
+            szs = [CAP + spill] + [CAP] * a
+        for c, p in zip(group, chunks(pool, szs)):
+            load[c] = p
+        helpers = ports + plain
+        back = {c: [] for c in helpers}
+        for x in selfs:
+            cand = [(len(back[c]) // 2, grow(load[c] + back[c], x), c) for c in helpers]
+            cand.sort()
+            back[cand[0][2]].append(x)
+        r1 = 128 // (16 // next_pow2(len(helpers)))
+        cost = r1 + 16 * len(load[me])
+        for c in helpers:
+            n = len(load[c])
+            cost = max(cost, r1 + 16 + (16 * n if n > CAP else (128 // (8 // next_pow2(n)) if n else 0)))
+        width = max(span(load[c] + back[c]) for c in helpers)
+        key = (cost, len(helpers), width)
+        if best is None or key < best[0]:
+            best = (key, load, back, helpers)
     return best
 
 
@@ -148,13 +122,11 @@ def build(tables, cores):
     arrive = {c: 0 for c in cores}
     for e in range(n):
         me = cores[e]
-        key, load, back, helpers, offs = assign(e, toks[e], me)
+        key, load, back, helpers = assign(e, toks[e], me)
         helpers = [c for c in helpers if load[c] or back[c]]
         width = max(span(load[c] + back[c]) for c in helpers)
-        order = [c for c in helpers if c in offs] + [c for c in helpers if c not in offs]
-        ms = masks_for(len(order), list(range(16)))
         hand[me] = []
-        for c, (m, cnt) in zip(order, ms):
+        for c, (m, cnt) in zip(helpers, masks_for(len(helpers), list(range(16)))):
             k0 = min(min(x[0] for x in load[c] + back[c]), ZCOLS - width)
             hand[me].append((c, k0, width, m))
             got[c] = cnt
@@ -164,9 +136,7 @@ def build(tables, cores):
             out = load[c]
             bk = back.get(c, [])
             cl = []
-            groups = [out]
-            if SPLIT_CALLS and len(out) > CAP:
-                groups = [out[i:i + CAP] for i in range(0, len(out), CAP)]
+            groups = [out[i:i + CAP] for i in range(0, len(out), CAP)] or [[]]
             for gi, grp in enumerate(groups):
                 trs = []
                 if grp:

import concourse.bass as bass

ZCOLS = 38
TOK = 32

SCRATCH = {
    "zs": ("sbuf", [128, ZCOLS], "float32"),
    "stage": ("sbuf", [128, TOK], "float32"),
}
SEMAPHORES = ["loaded", "got", "sent", "arrived", "stored"]

CAP = 4

PLAN = {}


def next_pow2(n):
    p = 1
    while p < n:
        p *= 2
    return p


def chunks(seq, sizes):
    out, i = [], 0
    for s in sizes:
        out.append(list(seq[i:i + s]))
        i += s
    return out


def even_sizes(n, parts):
    return [n // parts + (1 if i < n % parts else 0) for i in range(parts)]


def masks_for(n, engines):
    base = len(engines) // next_pow2(n)
    cnt = [base] * n
    spare = len(engines) - base * n
    for i in range(n):
        if spare >= cnt[i]:
            spare -= cnt[i]
            cnt[i] *= 2
    out, pos = [], 0
    for c in cnt:
        m = 0
        for x in engines[pos:pos + c]:
            m |= 1 << x
        pos += c
        out.append((m, c))
    return out


def span(toks):
    ks = [x[0] for x in toks]
    return (max(ks) - min(ks) + 1) if ks else 0


def grow(toks, tok):
    return span(toks + [tok]) - span(toks)


def assign(e, toks, me):
    base = me - 4
    other = [x for x in toks if x[1] % 2 != e % 2]
    same = [x for x in toks if x[1] % 2 == e % 2 and x[1] != e]
    selfs = [x for x in toks if x[1] == e]
    ports = [base + c for c in [6, 7, 2, 3]]
    best = None
    for a in range(3, -1, -1):
        plain = [base + c for c in [5, 0, 1][:a]]
        load = {}
        for c, p in zip(ports, chunks(other, even_sizes(len(other), 4))):
            load[c] = p
        spill = len(same) - min(len(same), (1 + a) * CAP)
        pool = list(same)
        while spill > 0:
            cand = [(grow(load[c], x), c, x) for c in ports if len(load[c]) < CAP for x in pool]
            if not cand:
                break
            cand.sort()
            c, x = cand[0][1], cand[0][2]
            load[c] = load[c] + [x]
            pool.remove(x)
            spill -= 1
        group = [me] + plain
        szs = even_sizes(len(pool), len(group))
        if spill > 0:
            szs = [CAP + spill] + [CAP] * a
        for c, p in zip(group, chunks(pool, szs)):
            load[c] = p
        helpers = ports + plain
        back = {c: [] for c in helpers}
        for x in selfs:
            cand = [(len(back[c]) // 2, grow(load[c] + back[c], x), c) for c in helpers]
            cand.sort()
            back[cand[0][2]].append(x)
        r1 = 128 // (16 // next_pow2(len(helpers)))
        cost = r1 + 16 * len(load[me])
        for c in helpers:
            n = len(load[c])
            cost = max(cost, r1 + 16 + (16 * n if n > CAP else (128 // (8 // next_pow2(n)) if n else 0)))
        width = max(span(load[c] + back[c]) for c in helpers)
        key = (cost, len(helpers), width)
        if best is None or key < best[0]:
            best = (key, load, back, helpers)
    return best


def build(tables, cores):
    route = tables["ROUTE"]
    n = len(cores)
    toks = [[] for i in range(n)]
    for r in range(n):
        for t in range(len(route[r])):
            e = route[r][t][0]
            toks[e].append((len(toks[e]), r, t))
    hand = {}
    got = {}
    first = {}
    calls = {}
    arrive = {c: 0 for c in cores}
    for e in range(n):
        me = cores[e]
        key, load, back, helpers = assign(e, toks[e], me)
        helpers = [c for c in helpers if load[c] or back[c]]
        width = max(span(load[c] + back[c]) for c in helpers)
        hand[me] = []
        for c, (m, cnt) in zip(helpers, masks_for(len(helpers), list(range(16)))):
            k0 = min(min(x[0] for x in load[c] + back[c]), ZCOLS - width)
            hand[me].append((c, k0, width, m))
            got[c] = cnt
            first[c] = k0
        first[me] = 0
        for c in [me] + helpers:
            out = load[c]
            bk = back.get(c, [])
            cl = []
            groups = [out[i:i + CAP] for i in range(0, len(out), CAP)] or [[]]
            for gi, grp in enumerate(groups):
                trs = []
                if grp:
                    for x, (m, cnt) in zip(grp, masks_for(len(grp), list(range(8)))):
                        trs.append((cores[x[1]], x[0] - first[c], x[2], m, cnt))
                if gi == 0 and bk:
                    for x, (m, cnt) in zip(bk, masks_for(len(bk), list(range(8, 16)))):
                        trs.append((cores[x[1]], x[0] - first[c], x[2], m, cnt))
                if trs:
                    cl.append(trs)
            calls[c] = cl
            for trs in cl:
                for d, kk, t, m, cnt in trs:
                    arrive[d] += cnt
    return {"hand": hand, "got": got, "calls": calls, "arrive": arrive}


def bits(m):
    return bin(m).count("1")


def rank_program(g, core, T, topo):
    if "p" not in PLAN:
        PLAN["p"] = build(T.tables, list(T.cores))
    p = PLAN["p"]
    rank = T.rank_of(core)
    if rank is None and core not in p["calls"]:
        return
    sent = 0

    if rank is not None:
        g.dma_start(T.zs[:, :], T.z[:, :]).then_inc(T.sem.loaded, 16)
        g.wait_ge(T.sem.loaded, 16)
        trs = []
        for c, k0, w, m in p["hand"][core]:
            rid, pid = topo.addr(c, core)
            trs.append(bass.RemoteDMATransfer(dst_ids=[bass.DstId(rid=rid, pnc=pid)], dma_engine_mask=m,
                                              remote_sem=T.sem.got, src=T.zs[:, k0:k0 + w], dst=T.zs[:, 0:w]))
            sent += bits(m)
        g.remote_dma_fused(trs, local_sem=T.sem.sent)
    else:
        g.wait_ge(T.sem.got, p["got"][core])

    for call in p["calls"][core]:
        trs = []
        for d, kk, t, m, cnt in call:
            rid, pid = topo.addr(d, core)
            trs.append(bass.RemoteDMATransfer(dst_ids=[bass.DstId(rid=rid, pnc=pid)], dma_engine_mask=m,
                                              remote_sem=T.sem.arrived, src=T.zs[:, kk:kk + 1], dst=T.stage[:, t:t + 1]))
            sent += cnt
        g.remote_dma_fused(trs, local_sem=T.sem.sent)

    if rank is not None:
        g.wait_ge(T.sem.arrived, p["arrive"][core])
        g.dma_start(T.y[:, :], T.stage[:, :]).then_inc(T.sem.stored, 16)
    g.wait_ge(T.sem.sent, sent)
    if rank is not None:
        g.wait_ge(T.sem.stored, 16)
